import numpy as np
import ml_dtypes


def mxq(x, axis, fmt="e4m3"):
    dtype, down = {"e4m3": (ml_dtypes.float8_e4m3fn, 7), "e5m2": (ml_dtypes.float8_e5m2, 14)}[fmt]
    v = np.moveaxis(np.asarray(x, np.float32).astype(ml_dtypes.bfloat16).astype(np.float64), axis, -1)
    blocks = v.reshape(v.shape[:-1] + (-1, 32))
    amax = np.abs(blocks).max(-1, keepdims=True)
    byte = np.maximum(np.where(amax > 0, np.frexp(amax)[1] - 1 + 127, 0) - down, 1)
    scale = np.exp2(byte - 127.0)
    codes = (blocks / scale).astype(np.float32).astype(dtype).astype(np.float64)
    return np.moveaxis((codes * scale).reshape(v.shape), -1, axis)


WIDE = False


def mx_kscale(k):
    if not WIDE:
        return np.ones(k)
    levels = np.array([10, -10, 5, -5, 0])
    if k % 512:
        return np.exp2(np.random.permutation(np.resize(levels, k // 32))).repeat(32)
    a = np.empty((k // 512, 16))
    for p in range(k // 512):
        a[p, :8] = np.random.permutation(np.resize(levels, 8))
        for g in range(8):
            far = levels[np.abs(levels - a[p, g]) >= 10]
            a[p, g + 8] = far[np.random.randint(len(far))]
    return np.exp2(a.ravel()).repeat(32)


def f64(x):
    return np.asarray(x).astype(np.float64)


def striped(idx):
    return np.tile(idx.reshape(-1, 16).T, (8, 1)).astype(np.uint16)


def unstriped(offs):
    return offs[:16].T.reshape(-1).astype(np.int64)


def pack_weight(w):
    k, n = w.shape
    w = f64(np.asarray(w, np.float32).astype(ml_dtypes.bfloat16)).reshape(k // 32, 32, n)
    amax = np.abs(w).max(1)
    byte = np.clip(np.where(amax > 0, np.frexp(amax)[1] - 1 + 127 - 7, 1), 1, 254)
    scaled = (w * np.exp2(127.0 - byte)[:, None, :]).reshape(k, n).astype(np.float32)
    words = np.ascontiguousarray(scaled.reshape(k // 512, 128, 4, n).transpose(0, 1, 3, 2)).astype(ml_dtypes.float8_e4m3fn).view(np.uint8)
    return words, np.ascontiguousarray(byte.astype(np.uint8).reshape(k // 512, 16, n))


def unpack_weight(words, scales):
    g, p, n, _ = words.shape
    vals = np.ascontiguousarray(words).view(ml_dtypes.float8_e4m3fn).astype(np.float64) * np.repeat(np.exp2(scales.astype(np.float64) - 127.0), 8, axis=1)[..., None]
    return vals.transpose(0, 1, 3, 2).reshape(g * 512, n)


K, T, S, D, N, H, V, U = 1024, 2048, 1024, 4, 256, 512, 256, 512


def setup_inputs():
    n = np.random.standard_normal
    s = mx_kscale(K)[:, None]
    u = mx_kscale(H)
    packed_xT = pack_weight(n((K, T)) * s)
    return {
        "x_words": packed_xT[0],
        "x_scales": packed_xT[1],
        "hT": (n((K, H)) / np.sqrt(K) / s).astype(np.float32),
        "tgt": (n((H, U))).astype(np.float32),
        "unit": (np.random.uniform(0.6, 1.4, (H, 1)) * u[:, None]).astype(np.float32),
        "w1": (n((H, N)) / np.sqrt(H) / u[:, None]).astype(np.float32),
        "offs": striped(np.random.permutation(T)[:S]),
        "use": striped(np.random.permutation(np.concatenate([np.arange(V), np.random.randint(0, V, U - V)]))),
    }


def reference(x_words, x_scales, hT, tgt, unit, w1, offs, use):
    hTq = mxq(f64(hT), 0, "e4m3")
    xq = unpack_weight(x_words, x_scales)[:, unstriped(offs)]
    y = hTq.T @ xq
    prtop = y.reshape(len(y), -1, D).max(axis=2)
    prexp = np.exp(y - np.repeat(prtop, D, axis=1))
    prsum = prexp.reshape(len(prexp), -1, D).sum(axis=2)
    pr = prexp / np.repeat(prsum, D, axis=1)
    py = pr * y
    ev = py.reshape(len(py), -1, D).sum(axis=2)
    eu = ev[:, unstriped(use)]
    p2 = (pr) ** 2
    conc = p2.reshape(len(p2), -1, D).sum(axis=2)
    hid = f64(unit) * (eu / (conc[:, unstriped(use)] + 0.5) - f64(tgt))
    return mxq(f64(w1), 0, "e4m3").T @ mxq(hid, 0, "e4m3")

@@ -1,0 +1,253 @@
+from contextlib import ExitStack
+
+import concourse.mybir as mybir
+from concourse.masks import make_identity
+
+K, T, S, D, N, H, V, U = 1024, 2048, 1024, 4, 256, 512, 256, 512
+FLOPS = 2 * K * H * S + 2 * H * N * U
+
+F32 = mybir.dt.float32
+BF16 = mybir.dt.bfloat16
+I32 = mybir.dt.int32
+U32 = mybir.dt.uint32
+U16 = mybir.dt.uint16
+U8 = mybir.dt.uint8
+FP8X4 = mybir.dt.float8_e4m3fn_x4
+ALU = mybir.AluOpType
+ACT = mybir.ActivationFunctionType
+AXIS = mybir.AxisListType
+
+P = 128
+PACK = 4
+K_PASS = P * PACK
+PASSES = K // K_PASS
+HALVES = V // P
+LIST_ROWS = 16
+
+
+def tile_picked_ycavqe_tgt_p_kernel(tc, x_words, x_scales, hT, tgt, unit, w1, offs, use, out):
+    nc = tc.nc
+    with ExitStack() as ctx:
+        keep = ctx.enter_context(tc.tile_pool(name="keep", bufs=1))
+        ring = ctx.enter_context(tc.tile_pool(name="ring", bufs=3))
+        score_banks = ctx.enter_context(tc.psum_pool(name="score_banks", bufs=4))
+        sum_banks = ctx.enter_context(tc.psum_pool(name="sum_banks", bufs=2))
+
+        offs_sb = keep.tile([P, S // LIST_ROWS], U16, name="offs_sb")
+        use_sb = keep.tile([P, U // LIST_ROWS], U16, name="use_sb")
+        table_words = [keep.tile([P, T], U32, name="table_words%d" % g, align_bytes=64) for g in range(PASSES)]
+        table_scales = keep.tile([P, T], U8, name="table_scales", align_bytes=64)
+        frame_pieces = [(0, 0, H), (1, 0, H // 2), (1, H // 2, H)]
+        frames_raw = [keep.tile([P, PACK, hi - lo], F32, name="frames_raw%d" % n) for n, (g, lo, hi) in enumerate(frame_pieces)]
+        tgt_raw = keep.tile([P, PACK, U], F32, name="tgt_raw")
+        unit_sb = keep.tile([P, PACK], F32, name="unit_sb")
+        w1_raw = keep.tile([P, PACK, N], F32, name="w1_raw")
+
+        def load_words(g):
+            nc.sync.dma_start(out=table_words[g][:].bitcast(I32), in_=x_words[g].rearrange("p n t -> p (n t)").bitcast(I32))
+
+        def load_frames(n):
+            g, lo, hi = frame_pieces[n]
+            rows = hT[g * K_PASS : (g + 1) * K_PASS, lo:hi]
+            nc.sync.dma_start(out=frames_raw[n][:], in_=rows.rearrange("(p j) f -> p j f", j=PACK))
+
+        nc.gpsimd.memset(table_scales[:].bitcast(I32), 0)
+        nc.sync.dma_start(out=offs_sb[:], in_=offs)
+        load_words(0)
+        for quad in range(4):
+            nc.sync.dma_start(
+                out=table_scales[32 * quad : 32 * quad + 4 * PASSES, :].bitcast(I32),
+                in_=x_scales[:, 4 * quad : 4 * quad + 4, :].bitcast(I32),
+            )
+        load_frames(0)
+        load_words(1)
+        load_frames(1)
+        load_frames(2)
+        nc.sync.dma_start(out=use_sb[:], in_=use)
+        nc.sync.dma_start(out=unit_sb[:], in_=unit.rearrange("(p t) o -> p (t o)", t=PACK))
+        nc.sync.dma_start(out=tgt_raw[:], in_=tgt.rearrange("(p t) r -> p t r", t=PACK))
+        nc.sync.dma_start(out=w1_raw[:], in_=w1.rearrange("(p j) m -> p j m", j=PACK))
+
+        ident = keep.tile([P, P], F32, name="ident")
+        make_identity(nc, ident[:])
+
+        picked_words = [[keep.tile([P, D, P], U32, name="picked_words%d_%d" % (g, h), align_bytes=64) for h in range(HALVES)] for g in range(PASSES)]
+        picked_scales = [keep.tile([P, D, P], U8, name="picked_scales%d" % h, align_bytes=64) for h in range(HALVES)]
+        half_cols = D * P // LIST_ROWS
+
+        def gather_words(g, h):
+            entries = offs_sb[:, h * half_cols : (h + 1) * half_cols]
+            nc.vector.tensor_copy(picked_words[g][h][:].rearrange("p d v -> p v d"), table_words[g][:].indirect(entries))
+
+        def gather_scales(h):
+            entries = offs_sb[:, h * half_cols : (h + 1) * half_cols]
+            nc.vector.tensor_copy(picked_scales[h][:].rearrange("p d v -> p v d"), table_scales[:].indirect(entries))
+
+        frames_bf = [keep.tile([P, H * PACK], BF16, name="frames_bf%d" % g, align_bytes=64) for g in range(PASSES)]
+        frame_codes = [keep.tile([P, H], U32, name="frame_codes%d" % g, align_bytes=64) for g in range(PASSES)]
+        frame_scales = [keep.tile([P, H], U8, name="frame_scales%d" % g, align_bytes=64) for g in range(PASSES)]
+
+        def round_frames(n, m_lo, m_hi, copy):
+            g, lo, hi = frame_pieces[n]
+            dst = frames_bf[g][:].rearrange("p (t m j) -> p m j t", t=PACK, j=PACK)
+            src = frames_raw[n][:].rearrange("p j (m t) -> p m j t", t=PACK)
+            copy(dst[:, lo // PACK + m_lo : lo // PACK + m_hi], src[:, m_lo:m_hi])
+
+        def quantize_frames(g, t_lo, t_hi):
+            nc.vector.quantize_mx(
+                out=frame_codes[g][:, t_lo * P : t_hi * P].bitcast(FP8X4),
+                scales=frame_scales[g][:, t_lo * P : t_hi * P],
+                in_=frames_bf[g][:, t_lo * P * PACK : t_hi * P * PACK],
+            )
+
+        for h in range(HALVES):
+            gather_words(0, h)
+        for h in range(HALVES):
+            gather_scales(h)
+        round_frames(0, 0, P, nc.scalar.copy)
+        gather_words(1, 0)
+        quantize_frames(0, 0, PACK)
+        gather_words(1, 1)
+        round_frames(1, 0, P // 2, nc.scalar.copy)
+        round_frames(2, 0, 24, nc.scalar.copy)
+        round_frames(2, 24, P // 2, nc.vector.tensor_copy)
+        quantize_frames(1, 0, 1)
+        quantize_frames(1, 1, PACK)
+
+        tgt_scaled = keep.tile([P, PACK, U], F32, name="tgt_scaled")
+        for t in range(PACK):
+            nc.gpsimd.tensor_scalar(tgt_scaled[:, t, :], tgt_raw[:, t, :], unit_sb[:, t : t + 1], 0.0, ALU.mult, ALU.add)
+        w1_bf = keep.tile([P, N * PACK], BF16, name="w1_bf", align_bytes=64)
+        w1_codes = keep.tile([P, N], U32, name="w1_codes", align_bytes=64)
+        w1_scales = keep.tile([P, N], U8, name="w1_scales", align_bytes=64)
+        nc.gpsimd.tensor_scalar(
+            w1_bf[:].rearrange("p (c i j) -> p c j i", i=4, j=PACK),
+            w1_raw[:].rearrange("p j (c i) -> p c j i", i=4),
+            1.0,
+            0.0,
+            ALU.mult,
+            ALU.add,
+        )
+
+        fetched = keep.tile([P, PACK, U], F32, name="fetched")
+        chunks = [(t, h) for t in range(PACK) for h in range(HALVES)]
+        state = {}
+
+        def scores(c):
+            t, h = chunks[c]
+            y = score_banks.tile([P, D, P], F32, name="bank")
+            for d in range(D):
+                for g in range(PASSES):
+                    nc.tensor.matmul_mx(
+                        out=y[:, d, :],
+                        lhsT=picked_words[g][h][:, d, :].bitcast(FP8X4),
+                        lhsT_scale=picked_scales[h][4 * g :, d, :],
+                        rhs=frame_codes[g][:, t * P : (t + 1) * P].bitcast(FP8X4),
+                        rhs_scale=frame_scales[g][:, t * P : (t + 1) * P],
+                        start=(g == 0),
+                        stop=(g == PASSES - 1),
+                    )
+            state[c, "y"] = y
+
+        def exponentials(c):
+            y = state[c, "y"]
+            top = ring.tile([P, P], F32, name="top")
+            nc.vector.tensor_reduce(top[:], y[:].rearrange("p d f -> p f d"), AXIS.X, ALU.max)
+            z = ring.tile([P, D, P], F32, name="z")
+            nc.vector.tensor_tensor(z[:], y[:], top[:].unsqueeze(1).to_broadcast([P, D, P]), ALU.subtract)
+            e = ring.tile([P, D, P], F32, name="e")
+            nc.scalar.activation(e[:], z[:], ACT.Exp)
+            e2 = ring.tile([P, D, P], F32, name="e2")
+            nc.scalar.activation(e2[:], z[:], ACT.Exp, scale=2.0)
+            state[c, "e"] = e
+            state[c, "e2"] = e2
+
+        def group_sums(c):
+            t, h = chunks[c]
+            ey = ring.tile([P, D, P], F32, name="ey")
+            nc.vector.tensor_tensor(ey[:], state[c, "y"][:], state[c, "e"][:], ALU.mult)
+            if h == 0:
+                state[t, "sums"] = sum_banks.tile([P, 2, V], F32, name="sums")
+                state[t, "weighted"] = sum_banks.tile([P, 2, V], F32, name="weighted")
+            cols = slice(h * P, (h + 1) * P)
+            targets = (
+                (state[c, "e"], state[t, "sums"][:, 0, cols]),
+                (state[c, "e2"], state[t, "sums"][:, 1, cols]),
+                (ey, state[t, "weighted"][:, 0, cols]),
+            )
+            for terms, total in targets:
+                for d in range(D):
+                    nc.tensor.matmul(total, terms[:, d, :], ident[:], start=(d == 0), stop=(d == D - 1), is_transpose=True)
+
+        def ratios(t):
+            sums, weighted = state[t, "sums"], state[t, "weighted"]
+            sum_sq = ring.tile([P, V], F32, name="sum_sq")
+            nc.scalar.activation(sum_sq[:], sums[:, 0, :], ACT.Square)
+            sum_twice = ring.tile([P, V], F32, name="sum_twice")
+            nc.scalar.activation(sum_twice[:], sums[:, 0, :], ACT.Copy, scale=2.0)
+            window = keep.tile([P, 4 * V], F32, name="window%d" % t)
+            ratio, num, den, crossed = [window[:, n * V : (n + 1) * V] for n in range(4)]
+            nc.vector.scalar_tensor_tensor(den, sums[:, 1, :], 2.0, sum_sq[:], ALU.mult, ALU.add)
+            nc.vector.scalar_tensor_tensor(num, weighted[:, 0, :], unit_sb[:, t : t + 1], sum_twice[:], ALU.mult, ALU.mult)
+            products = nc.vector
+            halves = lambda ap: ap.rearrange("p (a b) -> p a b", a=2)
+            pairs = ring.tile([P, V // 2], F32, name="pairs")
+            quads = ring.tile([P, V // 4], F32, name="quads")
+            inv_quads = ring.tile([P, V // 4], F32, name="inv_quads")
+            inv_pairs = ring.tile([P, V // 2], F32, name="inv_pairs")
+            products.tensor_tensor(pairs[:], den[:, : V // 2], den[:, V // 2 :], ALU.mult)
+            products.tensor_tensor(quads[:], pairs[:, : V // 4], pairs[:, V // 4 :], ALU.mult)
+            products.tensor_tensor(halves(crossed), halves(num), halves(den)[:, ::-1, :], ALU.mult)
+            nc.vector.reciprocal(inv_quads[:], quads[:])
+            products.tensor_tensor(
+                halves(inv_pairs[:]), halves(pairs[:])[:, ::-1, :], inv_quads[:].unsqueeze(1).to_broadcast([P, 2, V // 4]), ALU.mult
+            )
+            products.tensor_tensor(halves(ratio), halves(crossed), inv_pairs[:].unsqueeze(1).to_broadcast([P, 2, V // 2]), ALU.mult)
+            if t < PACK - 1:
+                nc.scalar.activation(fetched[:, t, :], window[:].indirect(use_sb[:]), ACT.Copy)
+            else:
+                cut = U // 2
+                nc.vector.tensor_copy(fetched[:, t, :cut], window[:].indirect(use_sb[:, : cut // LIST_ROWS]))
+                nc.scalar.activation(fetched[:, t, cut:], window[:].indirect(use_sb[:, cut // LIST_ROWS :]), ACT.Copy)
+
+        scores(0)
+        scores(1)
+        exponentials(0)
+        for c in range(len(chunks)):
+            if c + 2 < len(chunks):
+                scores(c + 2)
+            if c + 1 < len(chunks):
+                exponentials(c + 1)
+            group_sums(c)
+            if c == 1:
+                nc.vector.quantize_mx(out=w1_codes[:].bitcast(FP8X4), scales=w1_scales[:], in_=w1_bf[:])
+            if c % HALVES == 0 and c > 0:
+                ratios(c // HALVES - 1)
+        ratios(PACK - 1)
+
+        piece = U // 2
+        for r0 in range(0, U, piece):
+            hid_bf = ring.tile([P, piece * PACK], BF16, name="hid_bf", align_bytes=64)
+            nc.vector.tensor_tensor(
+                hid_bf[:].rearrange("p (c i t) -> p c t i", i=4, t=PACK),
+                fetched[:, :, r0 : r0 + piece].rearrange("p t (c i) -> p c t i", i=4),
+                tgt_scaled[:, :, r0 : r0 + piece].rearrange("p t (c i) -> p c t i", i=4),
+                ALU.subtract,
+            )
+            hid_codes = ring.tile([P, piece], U32, name="hid_codes", align_bytes=64)
+            hid_scales = ring.tile([P, piece], U8, name="hid_scales", align_bytes=64)
+            nc.vector.quantize_mx(out=hid_codes[:].bitcast(FP8X4), scales=hid_scales[:], in_=hid_bf[:])
+            acc = score_banks.tile([P, N // P, piece], F32, name="bank")
+            for mh in range(N // P):
+                nc.tensor.matmul_mx(
+                    out=acc[:, mh, :],
+                    lhsT=w1_codes[:, mh * P : (mh + 1) * P].bitcast(FP8X4),
+                    lhsT_scale=w1_scales[:, mh * P : (mh + 1) * P],
+                    rhs=hid_codes[:].bitcast(FP8X4),
+                    rhs_scale=hid_scales[:],
+                    start=True,
+                    stop=True,
+                )
+            result = ring.tile([P, N // P, piece], F32, name="result")
+            nc.scalar.copy(result[:], acc[:])
+            nc.sync.dma_start(out=out[:, r0 : r0 + piece].rearrange("(h p) r -> p h r", p=P), in_=result[:])

@@ -29,7 +29,7 @@ def tile_picked_ycavqe_tgt_p_kernel(tc, x_words, x_scales, hT, tgt, unit, w1, of
     nc = tc.nc
     with ExitStack() as ctx:
         keep = ctx.enter_context(tc.tile_pool(name="keep", bufs=1))
-        ring = ctx.enter_context(tc.tile_pool(name="ring", bufs=3))
+        ring = ctx.enter_context(tc.tile_pool(name="ring", bufs=5))
         score_banks = ctx.enter_context(tc.psum_pool(name="score_banks", bufs=4))
         sum_banks = ctx.enter_context(tc.psum_pool(name="sum_banks", bufs=2))
 
@@ -101,9 +101,9 @@ def tile_picked_ycavqe_tgt_p_kernel(tc, x_words, x_scales, hT, tgt, unit, w1, of
             )
 
         for h in range(HALVES):
-            gather_words(0, h)
-        for h in range(HALVES):
             gather_scales(h)
+        for h in range(HALVES):
+            gather_words(0, h)
         round_frames(0, 0, P, nc.scalar.copy)
         gather_words(1, 0)
         quantize_frames(0, 0, PACK)
@@ -132,6 +132,7 @@ def tile_picked_ycavqe_tgt_p_kernel(tc, x_words, x_scales, hT, tgt, unit, w1, of
         fetched = keep.tile([P, PACK, U], F32, name="fetched")
         chunks = [(t, h) for t in range(PACK) for h in range(HALVES)]
         state = {}
+        pieces = [(0, 128), (128, 384), (384, 512)]
 
         def scores(c):
             t, h = chunks[c]
@@ -157,8 +158,11 @@ def tile_picked_ycavqe_tgt_p_kernel(tc, x_words, x_scales, hT, tgt, unit, w1, of
             nc.vector.tensor_tensor(z[:], y[:], top[:].unsqueeze(1).to_broadcast([P, D, P]), ALU.subtract)
             e = ring.tile([P, D, P], F32, name="e")
             nc.scalar.activation(e[:], z[:], ACT.Exp)
-            e2 = ring.tile([P, D, P], F32, name="e2")
-            nc.scalar.activation(e2[:], z[:], ACT.Exp, scale=2.0)
+            if c % HALVES == 1 and c > 1:
+                e2 = fetched[:, c // HALVES - 1, :].rearrange("p (d f) -> p d f", d=D)
+            else:
+                e2 = ring.tile([P, D, P], F32, name="e2")[:]
+            nc.scalar.activation(e2, z[:], ACT.Exp, scale=2.0)
             state[c, "e"] = e
             state[c, "e2"] = e2
 
@@ -179,6 +183,27 @@ def tile_picked_ycavqe_tgt_p_kernel(tc, x_words, x_scales, hT, tgt, unit, w1, of
                 for d in range(D):
                     nc.tensor.matmul(total, terms[:, d, :], ident[:], start=(d == 0), stop=(d == D - 1), is_transpose=True)
 
+        def last_ratios(h):
+            t = PACK - 1
+            sums, weighted = state[t, "sums"], state[t, "weighted"]
+            cols = slice(h * P, (h + 1) * P)
+            sum_sq = ring.tile([P, P], F32, name="sum_sq")
+            nc.scalar.activation(sum_sq[:], sums[:, 0, cols], ACT.Square)
+            sum_twice = ring.tile([P, P], F32, name="sum_twice")
+            nc.scalar.activation(sum_twice[:], sums[:, 0, cols], ACT.Copy, scale=2.0)
+            if h == 0:
+                state[t, "window"] = keep.tile([P, 4 * V], F32, name="window%d" % t)
+            ratio, num, den, crossed = [state[t, "window"][:, n * V + h * P : n * V + (h + 1) * P] for n in range(4)]
+            nc.vector.scalar_tensor_tensor(den, sums[:, 1, cols], 2.0, sum_sq[:], ALU.mult, ALU.add)
+            nc.vector.scalar_tensor_tensor(num, weighted[:, 0, cols], unit_sb[:, t : t + 1], sum_twice[:], ALU.mult, ALU.mult)
+            halves = lambda ap: ap.rearrange("p (a b) -> p a b", a=2)
+            pairs = ring.tile([P, P // 2], F32, name="pairs")
+            inv_pairs = ring.tile([P, P // 2], F32, name="inv_pairs")
+            nc.vector.tensor_tensor(pairs[:], den[:, : P // 2], den[:, P // 2 :], ALU.mult)
+            nc.vector.reciprocal(inv_pairs[:], pairs[:])
+            nc.vector.tensor_tensor(halves(crossed), halves(num), halves(den)[:, ::-1, :], ALU.mult)
+            nc.vector.tensor_tensor(halves(ratio), halves(crossed), inv_pairs[:].unsqueeze(1).to_broadcast([P, 2, P // 2]), ALU.mult)
+
         def ratios(t):
             sums, weighted = state[t, "sums"], state[t, "weighted"]
             sum_sq = ring.tile([P, V], F32, name="sum_sq")
@@ -189,7 +214,7 @@ def tile_picked_ycavqe_tgt_p_kernel(tc, x_words, x_scales, hT, tgt, unit, w1, of
             ratio, num, den, crossed = [window[:, n * V : (n + 1) * V] for n in range(4)]
             nc.vector.scalar_tensor_tensor(den, sums[:, 1, :], 2.0, sum_sq[:], ALU.mult, ALU.add)
             nc.vector.scalar_tensor_tensor(num, weighted[:, 0, :], unit_sb[:, t : t + 1], sum_twice[:], ALU.mult, ALU.mult)
-            products = nc.vector
+            products = nc.gpsimd
             halves = lambda ap: ap.rearrange("p (a b) -> p a b", a=2)
             pairs = ring.tile([P, V // 2], F32, name="pairs")
             quads = ring.tile([P, V // 4], F32, name="quads")
@@ -203,12 +228,15 @@ def tile_picked_ycavqe_tgt_p_kernel(tc, x_words, x_scales, hT, tgt, unit, w1, of
                 halves(inv_pairs[:]), halves(pairs[:])[:, ::-1, :], inv_quads[:].unsqueeze(1).to_broadcast([P, 2, V // 4]), ALU.mult
             )
             products.tensor_tensor(halves(ratio), halves(crossed), inv_pairs[:].unsqueeze(1).to_broadcast([P, 2, V // 2]), ALU.mult)
+            state[t, "window"] = window
+
+        def fetch(t):
+            window = state[t, "window"]
             if t < PACK - 1:
                 nc.scalar.activation(fetched[:, t, :], window[:].indirect(use_sb[:]), ACT.Copy)
             else:
-                cut = U // 2
-                nc.vector.tensor_copy(fetched[:, t, :cut], window[:].indirect(use_sb[:, : cut // LIST_ROWS]))
-                nc.scalar.activation(fetched[:, t, cut:], window[:].indirect(use_sb[:, cut // LIST_ROWS :]), ACT.Copy)
+                for lo, hi in pieces:
+                    nc.scalar.activation(fetched[:, t, lo:hi], window[:].indirect(use_sb[:, lo // LIST_ROWS : hi // LIST_ROWS]), ACT.Copy)
 
         scores(0)
         scores(1)
@@ -223,10 +251,14 @@ def tile_picked_ycavqe_tgt_p_kernel(tc, x_words, x_scales, hT, tgt, unit, w1, of
                 nc.vector.quantize_mx(out=w1_codes[:].bitcast(FP8X4), scales=w1_scales[:], in_=w1_bf[:])
             if c % HALVES == 0 and c > 0:
                 ratios(c // HALVES - 1)
-        ratios(PACK - 1)
+            if c % HALVES == 1 and c > 1:
+                fetch(c // HALVES - 1)
+            if chunks[c][0] == PACK - 1:
+                last_ratios(chunks[c][1])
+        fetch(PACK - 1)
 
-        piece = U // 2
-        for r0 in range(0, U, piece):
+        for r0, r1 in pieces:
+            piece = r1 - r0
             hid_bf = ring.tile([P, piece * PACK], BF16, name="hid_bf", align_bytes=64)
             nc.vector.tensor_tensor(
                 hid_bf[:].rearrange("p (c i t) -> p c t i", i=4, t=PACK),

@@ -23,6 +23,11 @@ K_PASS = P * PACK
 PASSES = K // K_PASS
 HALVES = V // P
 LIST_ROWS = 16
+LAG = 1
+FETCH_AFTER = [5, 7]
+SQUARE_AFTER = [2, 4, 6]
+INVERT_AFTER = [4, 6, 7]
+GPSIMD_TILES = 2
 
 
 def tile_picked_ycavqe_tgt_p_kernel(tc, x_words, x_scales, hT, tgt, unit, w1, offs, use, out):
@@ -137,32 +142,34 @@ def tile_picked_ycavqe_tgt_p_kernel(tc, x_words, x_scales, hT, tgt, unit, w1, of
         def scores(c):
             t, h = chunks[c]
             y = score_banks.tile([P, D, P], F32, name="bank")
-            for d in range(D):
-                for g in range(PASSES):
+            for g in range(PASSES):
+                for d in range(D):
                     nc.tensor.matmul_mx(
                         out=y[:, d, :],
                         lhsT=picked_words[g][h][:, d, :].bitcast(FP8X4),
                         lhsT_scale=picked_scales[h][4 * g :, d, :],
                         rhs=frame_codes[g][:, t * P : (t + 1) * P].bitcast(FP8X4),
                         rhs_scale=frame_scales[g][:, t * P : (t + 1) * P],
-                        start=(g == 0),
-                        stop=(g == PASSES - 1),
+                        start=(g == 0 and d == 0),
+                        stop=(g == PASSES - 1 and d == D - 1),
                     )
             state[c, "y"] = y
 
         def exponentials(c):
             y = state[c, "y"]
-            top = ring.tile([P, P], F32, name="top")
+            top = keep.tile([P, P], F32, name="top%d" % c)
+            state[c, "top"] = top
             nc.vector.tensor_reduce(top[:], y[:].rearrange("p d f -> p f d"), AXIS.X, ALU.max)
-            z = ring.tile([P, D, P], F32, name="z")
-            nc.vector.tensor_tensor(z[:], y[:], top[:].unsqueeze(1).to_broadcast([P, D, P]), ALU.subtract)
-            e = ring.tile([P, D, P], F32, name="e")
-            nc.scalar.activation(e[:], z[:], ACT.Exp)
-            if c % HALVES == 1 and c > 1:
-                e2 = fetched[:, c // HALVES - 1, :].rearrange("p (d f) -> p d f", d=D)
+            if c in FETCH_AFTER:
+                z = fetched[:, FETCH_AFTER.index(c), :].rearrange("p (d f) -> p d f", d=D)
             else:
-                e2 = ring.tile([P, D, P], F32, name="e2")[:]
-            nc.scalar.activation(e2, z[:], ACT.Exp, scale=2.0)
+                z = keep.tile([P, D, P], F32, name="z%d" % c)[:]
+            state[c, "z"] = z
+            nc.vector.tensor_tensor(z, y[:], top[:].unsqueeze(1).to_broadcast([P, D, P]), ALU.subtract)
+            e = ring.tile([P, D, P], F32, name="e")
+            nc.scalar.activation(e[:], z, ACT.Exp)
+            e2 = ring.tile([P, D, P], F32, name="e2")
+            nc.scalar.activation(e2[:], z, ACT.Exp, scale=2.0)
             state[c, "e"] = e
             state[c, "e2"] = e2
 
@@ -174,28 +181,29 @@ def tile_picked_ycavqe_tgt_p_kernel(tc, x_words, x_scales, hT, tgt, unit, w1, of
                 state[t, "sums"] = sum_banks.tile([P, 2, V], F32, name="sums")
                 state[t, "weighted"] = sum_banks.tile([P, 2, V], F32, name="weighted")
             cols = slice(h * P, (h + 1) * P)
-            targets = (
-                (state[c, "e"], state[t, "sums"][:, 0, cols]),
-                (state[c, "e2"], state[t, "sums"][:, 1, cols]),
-                (ey, state[t, "weighted"][:, 0, cols]),
-            )
+            totals = [state[t, "sums"][:, 0, cols], state[t, "sums"][:, 1, cols], state[t, "weighted"][:, 0, cols]]
+            if c == len(chunks) - 1:
+                spare_sums = score_banks.tile([P, D, P], F32, name="bank")
+                spare_weighted = score_banks.tile([P, D, P], F32, name="bank")
+                totals = [spare_sums[:, 0, :], spare_sums[:, 1, :], spare_weighted[:, 0, :]]
+            state[c, "totals"] = totals
+            targets = zip((state[c, "e"], state[c, "e2"], ey), totals)
             for terms, total in targets:
                 for d in range(D):
                     nc.tensor.matmul(total, terms[:, d, :], ident[:], start=(d == 0), stop=(d == D - 1), is_transpose=True)
 
         def last_ratios(h):
             t = PACK - 1
-            sums, weighted = state[t, "sums"], state[t, "weighted"]
-            cols = slice(h * P, (h + 1) * P)
+            sum_e, sum_e2, sum_ey = state[HALVES * t + h, "totals"]
             sum_sq = ring.tile([P, P], F32, name="sum_sq")
-            nc.scalar.activation(sum_sq[:], sums[:, 0, cols], ACT.Square)
+            nc.scalar.activation(sum_sq[:], sum_e, ACT.Square)
             sum_twice = ring.tile([P, P], F32, name="sum_twice")
-            nc.scalar.activation(sum_twice[:], sums[:, 0, cols], ACT.Copy, scale=2.0)
+            nc.scalar.activation(sum_twice[:], sum_e, ACT.Copy, scale=2.0)
             if h == 0:
                 state[t, "window"] = keep.tile([P, 4 * V], F32, name="window%d" % t)
             ratio, num, den, crossed = [state[t, "window"][:, n * V + h * P : n * V + (h + 1) * P] for n in range(4)]
-            nc.vector.scalar_tensor_tensor(den, sums[:, 1, cols], 2.0, sum_sq[:], ALU.mult, ALU.add)
-            nc.vector.scalar_tensor_tensor(num, weighted[:, 0, cols], unit_sb[:, t : t + 1], sum_twice[:], ALU.mult, ALU.mult)
+            nc.vector.scalar_tensor_tensor(den, sum_e2, 2.0, sum_sq[:], ALU.mult, ALU.add)
+            nc.vector.scalar_tensor_tensor(num, sum_ey, unit_sb[:, t : t + 1], sum_twice[:], ALU.mult, ALU.mult)
             halves = lambda ap: ap.rearrange("p (a b) -> p a b", a=2)
             pairs = ring.tile([P, P // 2], F32, name="pairs")
             inv_pairs = ring.tile([P, P // 2], F32, name="inv_pairs")
@@ -206,19 +214,19 @@ def tile_picked_ycavqe_tgt_p_kernel(tc, x_words, x_scales, hT, tgt, unit, w1, of
 
         def ratios(t):
             sums, weighted = state[t, "sums"], state[t, "weighted"]
-            sum_sq = ring.tile([P, V], F32, name="sum_sq")
-            nc.scalar.activation(sum_sq[:], sums[:, 0, :], ACT.Square)
-            sum_twice = ring.tile([P, V], F32, name="sum_twice")
-            nc.scalar.activation(sum_twice[:], sums[:, 0, :], ACT.Copy, scale=2.0)
+            spent = state[SQUARE_AFTER[t], "z"].rearrange("p d f -> p (d f)")
+            sum_sq, sum_twice = spent[:, :V], spent[:, V:]
+            nc.scalar.activation(sum_sq, sums[:, 0, :], ACT.Square)
+            nc.scalar.activation(sum_twice, sums[:, 0, :], ACT.Copy, scale=2.0)
             window = keep.tile([P, 4 * V], F32, name="window%d" % t)
             ratio, num, den, crossed = [window[:, n * V : (n + 1) * V] for n in range(4)]
             nc.vector.scalar_tensor_tensor(den, sums[:, 1, :], 2.0, sum_sq[:], ALU.mult, ALU.add)
             nc.vector.scalar_tensor_tensor(num, weighted[:, 0, :], unit_sb[:, t : t + 1], sum_twice[:], ALU.mult, ALU.mult)
-            products = nc.gpsimd
+            products = nc.gpsimd if t < GPSIMD_TILES else nc.vector
             halves = lambda ap: ap.rearrange("p (a b) -> p a b", a=2)
             pairs = ring.tile([P, V // 2], F32, name="pairs")
             quads = ring.tile([P, V // 4], F32, name="quads")
-            inv_quads = ring.tile([P, V // 4], F32, name="inv_quads")
+            inv_quads = state[INVERT_AFTER[t], "top"][:, (t % 2) * V // 4 : (t % 2 + 1) * V // 4]
             inv_pairs = ring.tile([P, V // 2], F32, name="inv_pairs")
             products.tensor_tensor(pairs[:], den[:, : V // 2], den[:, V // 2 :], ALU.mult)
             products.tensor_tensor(quads[:], pairs[:, : V // 4], pairs[:, V // 4 :], ALU.mult)
@@ -238,24 +246,25 @@ def tile_picked_ycavqe_tgt_p_kernel(tc, x_words, x_scales, hT, tgt, unit, w1, of
                 for lo, hi in pieces:
                     nc.scalar.activation(fetched[:, t, lo:hi], window[:].indirect(use_sb[:, lo // LIST_ROWS : hi // LIST_ROWS]), ACT.Copy)
 
+        last = len(chunks) - 1
         scores(0)
-        scores(1)
-        exponentials(0)
-        for c in range(len(chunks)):
-            if c + 2 < len(chunks):
-                scores(c + 2)
-            if c + 1 < len(chunks):
-                exponentials(c + 1)
-            group_sums(c)
-            if c == 1:
-                nc.vector.quantize_mx(out=w1_codes[:].bitcast(FP8X4), scales=w1_scales[:], in_=w1_bf[:])
-            if c % HALVES == 0 and c > 0:
-                ratios(c // HALVES - 1)
-            if c % HALVES == 1 and c > 1:
-                fetch(c // HALVES - 1)
-            if chunks[c][0] == PACK - 1:
+        for step in range(len(chunks) + LAG):
+            if step < last:
+                scores(step + 1)
+            if step <= last:
+                exponentials(step)
+            c = step - LAG
+            if c >= 0:
+                group_sums(c)
+            for t in range(PACK - 1):
+                if min(step, last) == last or step == INVERT_AFTER[t]:
+                    if (t, "window") not in state and c >= HALVES * t + 1:
+                        ratios(t)
+            if c >= 0 and chunks[c][0] == PACK - 1:
                 last_ratios(chunks[c][1])
-        fetch(PACK - 1)
+        nc.vector.quantize_mx(out=w1_codes[:].bitcast(FP8X4), scales=w1_scales[:], in_=w1_bf[:])
+        for t in range(PACK):
+            fetch(t)
 
         for r0, r1 in pieces:
             piece = r1 - r0

@@ -43,7 +43,7 @@ def tile_picked_ycavqe_tgt_p_kernel(tc, x_words, x_scales, hT, tgt, unit, w1, of
         table_words = [keep.tile([P, T], U32, name="table_words%d" % g, align_bytes=64) for g in range(PASSES)]
         table_scales = keep.tile([P, T], U8, name="table_scales", align_bytes=64)
         frame_pieces = [(0, 0, H), (1, 0, H // 2), (1, H // 2, H)]
-        frames_raw = [keep.tile([P, PACK, hi - lo], F32, name="frames_raw%d" % n) for n, (g, lo, hi) in enumerate(frame_pieces)]
+        frames_raw = [keep.tile([P, PACK, hi - lo], F32, name="frames_raw%d" % n, tag="frames_raw%d" % n, align_bytes=64) for n, (g, lo, hi) in enumerate(frame_pieces)]
         tgt_raw = keep.tile([P, PACK, U], F32, name="tgt_raw")
         unit_sb = keep.tile([P, PACK], F32, name="unit_sb")
         w1_raw = keep.tile([P, PACK, N], F32, name="w1_raw")
@@ -76,48 +76,50 @@ def tile_picked_ycavqe_tgt_p_kernel(tc, x_words, x_scales, hT, tgt, unit, w1, of
         ident = keep.tile([P, P], F32, name="ident")
         make_identity(nc, ident[:])
 
-        picked_words = [[keep.tile([P, D, P], U32, name="picked_words%d_%d" % (g, h), align_bytes=64) for h in range(HALVES)] for g in range(PASSES)]
+        picked_words = {}
         picked_scales = [keep.tile([P, D, P], U8, name="picked_scales%d" % h, align_bytes=64) for h in range(HALVES)]
         half_cols = D * P // LIST_ROWS
 
-        def gather_words(g, h):
+        def gather_words(g, h, slot):
+            picked_words[g, h] = keep.tile([P, D, P], U32, name="picked_words%d_%d" % (g, h), tag=slot, align_bytes=64)
             entries = offs_sb[:, h * half_cols : (h + 1) * half_cols]
-            nc.vector.tensor_copy(picked_words[g][h][:].rearrange("p d v -> p v d"), table_words[g][:].indirect(entries))
+            nc.vector.tensor_copy(picked_words[g, h][:].rearrange("p d v -> p v d"), table_words[g][:].indirect(entries))
 
         def gather_scales(h):
             entries = offs_sb[:, h * half_cols : (h + 1) * half_cols]
             nc.vector.tensor_copy(picked_scales[h][:].rearrange("p d v -> p v d"), table_scales[:].indirect(entries))
 
-        frames_bf = [keep.tile([P, H * PACK], BF16, name="frames_bf%d" % g, align_bytes=64) for g in range(PASSES)]
-        frame_codes = [keep.tile([P, H], U32, name="frame_codes%d" % g, align_bytes=64) for g in range(PASSES)]
-        frame_scales = [keep.tile([P, H], U8, name="frame_scales%d" % g, align_bytes=64) for g in range(PASSES)]
+        frames_bf = keep.tile([P, PASSES * H * PACK], BF16, name="frames_bf", align_bytes=64)
+        frame_codes = keep.tile([P, PASSES * H], U32, name="frame_codes", align_bytes=64)
+        frame_scales = keep.tile([P, PASSES * H], U8, name="frame_scales", align_bytes=64)
 
         def round_frames(n, m_lo, m_hi, copy):
             g, lo, hi = frame_pieces[n]
-            dst = frames_bf[g][:].rearrange("p (t m j) -> p m j t", t=PACK, j=PACK)
+            dst = frames_bf[:].rearrange("p (t g m j) -> p g m j t", t=PACK, g=PASSES, j=PACK)[:, g]
             src = frames_raw[n][:].rearrange("p j (m t) -> p m j t", t=PACK)
             copy(dst[:, lo // PACK + m_lo : lo // PACK + m_hi], src[:, m_lo:m_hi])
 
-        def quantize_frames(g, t_lo, t_hi):
+        def quantize_frames(t_lo, t_hi):
+            lo, hi = t_lo * PASSES * P, t_hi * PASSES * P
             nc.vector.quantize_mx(
-                out=frame_codes[g][:, t_lo * P : t_hi * P].bitcast(FP8X4),
-                scales=frame_scales[g][:, t_lo * P : t_hi * P],
-                in_=frames_bf[g][:, t_lo * P * PACK : t_hi * P * PACK],
+                out=frame_codes[:, lo:hi].bitcast(FP8X4),
+                scales=frame_scales[:, lo:hi],
+                in_=frames_bf[:, lo * PACK : hi * PACK],
             )
 
         for h in range(HALVES):
             gather_scales(h)
         for h in range(HALVES):
-            gather_words(0, h)
+            gather_words(0, h, "picked_words0_%d" % h)
         round_frames(0, 0, P, nc.scalar.copy)
-        gather_words(1, 0)
-        quantize_frames(0, 0, PACK)
-        gather_words(1, 1)
+        gather_words(1, 0, "picked_words1_0")
         round_frames(1, 0, P // 2, nc.scalar.copy)
         round_frames(2, 0, 24, nc.scalar.copy)
         round_frames(2, 24, P // 2, nc.vector.tensor_copy)
-        quantize_frames(1, 0, 1)
-        quantize_frames(1, 1, PACK)
+        quantize_frames(0, 1)
+        gather_words(1, 1, "frames_raw2")
+        quantize_frames(1, 2)
+        quantize_frames(2, PACK)
 
         tgt_scaled = keep.tile([P, PACK, U], F32, name="tgt_scaled")
         for t in range(PACK):
@@ -126,8 +128,8 @@ def tile_picked_ycavqe_tgt_p_kernel(tc, x_words, x_scales, hT, tgt, unit, w1, of
         w1_codes = keep.tile([P, N], U32, name="w1_codes", align_bytes=64)
         w1_scales = keep.tile([P, N], U8, name="w1_scales", align_bytes=64)
         nc.gpsimd.tensor_scalar(
-            w1_bf[:].rearrange("p (c i j) -> p c j i", i=4, j=PACK),
-            w1_raw[:].rearrange("p j (c i) -> p c j i", i=4),
+            w1_bf[:].rearrange("p (m j) -> p m j", j=PACK),
+            w1_raw[:].rearrange("p j m -> p m j"),
             1.0,
             0.0,
             ALU.mult,
@@ -143,13 +145,14 @@ def tile_picked_ycavqe_tgt_p_kernel(tc, x_words, x_scales, hT, tgt, unit, w1, of
             t, h = chunks[c]
             y = score_banks.tile([P, D, P], F32, name="bank")
             for g in range(PASSES):
+                moving = slice((t * PASSES + g) * P, (t * PASSES + g + 1) * P)
                 for d in range(D):
                     nc.tensor.matmul_mx(
                         out=y[:, d, :],
-                        lhsT=picked_words[g][h][:, d, :].bitcast(FP8X4),
+                        lhsT=picked_words[g, h][:, d, :].bitcast(FP8X4),
                         lhsT_scale=picked_scales[h][4 * g :, d, :],
-                        rhs=frame_codes[g][:, t * P : (t + 1) * P].bitcast(FP8X4),
-                        rhs_scale=frame_scales[g][:, t * P : (t + 1) * P],
+                        rhs=frame_codes[:, moving].bitcast(FP8X4),
+                        rhs_scale=frame_scales[:, moving],
                         start=(g == 0 and d == 0),
                         stop=(g == PASSES - 1 and d == D - 1),
                     )

from contextlib import ExitStack

import concourse.mybir as mybir
from concourse.masks import make_identity

K, T, S, D, N, H, V, U = 1024, 2048, 1024, 4, 256, 512, 256, 512
FLOPS = 2 * K * H * S + 2 * H * N * U

F32 = mybir.dt.float32
BF16 = mybir.dt.bfloat16
I32 = mybir.dt.int32
U32 = mybir.dt.uint32
U16 = mybir.dt.uint16
U8 = mybir.dt.uint8
FP8X4 = mybir.dt.float8_e4m3fn_x4
ALU = mybir.AluOpType
ACT = mybir.ActivationFunctionType
AXIS = mybir.AxisListType

P = 128
PACK = 4
K_PASS = P * PACK
PASSES = K // K_PASS
HALVES = V // P
LIST_ROWS = 16
LAG = 1
FETCH_AFTER = [5, 7]
SQUARE_AFTER = [2, 4, 6]
INVERT_AFTER = [4, 6, 7]
GPSIMD_TILES = 2


def tile_picked_ycavqe_tgt_p_kernel(tc, x_words, x_scales, hT, tgt, unit, w1, offs, use, out):
    nc = tc.nc
    with ExitStack() as ctx:
        keep = ctx.enter_context(tc.tile_pool(name="keep", bufs=1))
        ring = ctx.enter_context(tc.tile_pool(name="ring", bufs=5))
        score_banks = ctx.enter_context(tc.psum_pool(name="score_banks", bufs=4))
        sum_banks = ctx.enter_context(tc.psum_pool(name="sum_banks", bufs=2))

        offs_sb = keep.tile([P, S // LIST_ROWS], U16, name="offs_sb")
        use_sb = keep.tile([P, U // LIST_ROWS], U16, name="use_sb")
        table_words = [keep.tile([P, T], U32, name="table_words%d" % g, align_bytes=64) for g in range(PASSES)]
        table_scales = keep.tile([P, T], U8, name="table_scales", align_bytes=64)
        frame_pieces = [(0, 0, H), (1, 0, H // 2), (1, H // 2, H)]
        frames_raw = [keep.tile([P, PACK, hi - lo], F32, name="frames_raw%d" % n, tag="frames_raw%d" % n, align_bytes=64) for n, (g, lo, hi) in enumerate(frame_pieces)]
        tgt_raw = keep.tile([P, PACK, U], F32, name="tgt_raw")
        unit_sb = keep.tile([P, PACK], F32, name="unit_sb")
        w1_raw = keep.tile([P, PACK, N], F32, name="w1_raw")

        def load_words(g):
            nc.sync.dma_start(out=table_words[g][:].bitcast(I32), in_=x_words[g].rearrange("p n t -> p (n t)").bitcast(I32))

        def load_frames(n):
            g, lo, hi = frame_pieces[n]
            rows = hT[g * K_PASS : (g + 1) * K_PASS, lo:hi]
            nc.sync.dma_start(out=frames_raw[n][:], in_=rows.rearrange("(p j) f -> p j f", j=PACK))

        nc.gpsimd.memset(table_scales[:].bitcast(I32), 0)
        nc.sync.dma_start(out=offs_sb[:], in_=offs)
        load_words(0)
        for quad in range(4):
            nc.sync.dma_start(
                out=table_scales[32 * quad : 32 * quad + 4 * PASSES, :].bitcast(I32),
                in_=x_scales[:, 4 * quad : 4 * quad + 4, :].bitcast(I32),
            )
        load_frames(0)
        load_words(1)
        load_frames(1)
        load_frames(2)
        nc.sync.dma_start(out=use_sb[:], in_=use)
        nc.sync.dma_start(out=unit_sb[:], in_=unit.rearrange("(p t) o -> p (t o)", t=PACK))
        nc.sync.dma_start(out=tgt_raw[:], in_=tgt.rearrange("(p t) r -> p t r", t=PACK))
        nc.sync.dma_start(out=w1_raw[:], in_=w1.rearrange("(p j) m -> p j m", j=PACK))

        ident = keep.tile([P, P], F32, name="ident")
        make_identity(nc, ident[:])

        picked_words = {}
        picked_scales = [keep.tile([P, D, P], U8, name="picked_scales%d" % h, align_bytes=64) for h in range(HALVES)]
        half_cols = D * P // LIST_ROWS

        def gather_words(g, h, slot):
            picked_words[g, h] = keep.tile([P, D, P], U32, name="picked_words%d_%d" % (g, h), tag=slot, align_bytes=64)
            entries = offs_sb[:, h * half_cols : (h + 1) * half_cols]
            nc.vector.tensor_copy(picked_words[g, h][:].rearrange("p d v -> p v d"), table_words[g][:].indirect(entries))

        def gather_scales(h):
            entries = offs_sb[:, h * half_cols : (h + 1) * half_cols]
            nc.vector.tensor_copy(picked_scales[h][:].rearrange("p d v -> p v d"), table_scales[:].indirect(entries))

        frames_bf = keep.tile([P, PASSES * H * PACK], BF16, name="frames_bf", align_bytes=64)
        frame_codes = keep.tile([P, PASSES * H], U32, name="frame_codes", align_bytes=64)
        frame_scales = keep.tile([P, PASSES * H], U8, name="frame_scales", align_bytes=64)

        def round_frames(n, m_lo, m_hi, copy):
            g, lo, hi = frame_pieces[n]
            dst = frames_bf[:].rearrange("p (t g m j) -> p g m j t", t=PACK, g=PASSES, j=PACK)[:, g]
            src = frames_raw[n][:].rearrange("p j (m t) -> p m j t", t=PACK)
            copy(dst[:, lo // PACK + m_lo : lo // PACK + m_hi], src[:, m_lo:m_hi])

        def quantize_frames(t_lo, t_hi):
            lo, hi = t_lo * PASSES * P, t_hi * PASSES * P
            nc.vector.quantize_mx(
                out=frame_codes[:, lo:hi].bitcast(FP8X4),
                scales=frame_scales[:, lo:hi],
                in_=frames_bf[:, lo * PACK : hi * PACK],
            )

        for h in range(HALVES):
            gather_scales(h)
        for h in range(HALVES):
            gather_words(0, h, "picked_words0_%d" % h)
        round_frames(0, 0, P, nc.scalar.copy)
        gather_words(1, 0, "picked_words1_0")
        round_frames(1, 0, P // 2, nc.scalar.copy)
        round_frames(2, 0, 24, nc.scalar.copy)
        round_frames(2, 24, P // 2, nc.vector.tensor_copy)
        quantize_frames(0, 1)
        gather_words(1, 1, "frames_raw2")
        quantize_frames(1, 2)
        quantize_frames(2, PACK)

        tgt_scaled = keep.tile([P, PACK, U], F32, name="tgt_scaled")
        for t in range(PACK):
            nc.gpsimd.tensor_scalar(tgt_scaled[:, t, :], tgt_raw[:, t, :], unit_sb[:, t : t + 1], 0.0, ALU.mult, ALU.add)
        w1_bf = keep.tile([P, N * PACK], BF16, name="w1_bf", align_bytes=64)
        w1_codes = keep.tile([P, N], U32, name="w1_codes", align_bytes=64)
        w1_scales = keep.tile([P, N], U8, name="w1_scales", align_bytes=64)
        nc.gpsimd.tensor_scalar(
            w1_bf[:].rearrange("p (m j) -> p m j", j=PACK),
            w1_raw[:].rearrange("p j m -> p m j"),
            1.0,
            0.0,
            ALU.mult,
            ALU.add,
        )

        fetched = keep.tile([P, PACK, U], F32, name="fetched")
        chunks = [(t, h) for t in range(PACK) for h in range(HALVES)]
        state = {}
        pieces = [(0, 128), (128, 384), (384, 512)]

        def scores(c):
            t, h = chunks[c]
            y = score_banks.tile([P, D, P], F32, name="bank")
            for g in range(PASSES):
                moving = slice((t * PASSES + g) * P, (t * PASSES + g + 1) * P)
                for d in range(D):
                    nc.tensor.matmul_mx(
                        out=y[:, d, :],
                        lhsT=picked_words[g, h][:, d, :].bitcast(FP8X4),
                        lhsT_scale=picked_scales[h][4 * g :, d, :],
                        rhs=frame_codes[:, moving].bitcast(FP8X4),
                        rhs_scale=frame_scales[:, moving],
                        start=(g == 0 and d == 0),
                        stop=(g == PASSES - 1 and d == D - 1),
                    )
            state[c, "y"] = y

        def exponentials(c):
            y = state[c, "y"]
            top = keep.tile([P, P], F32, name="top%d" % c)
            state[c, "top"] = top
            nc.vector.tensor_reduce(top[:], y[:].rearrange("p d f -> p f d"), AXIS.X, ALU.max)
            if c in FETCH_AFTER:
                z = fetched[:, FETCH_AFTER.index(c), :].rearrange("p (d f) -> p d f", d=D)
            else:
                z = keep.tile([P, D, P], F32, name="z%d" % c)[:]
            state[c, "z"] = z
            nc.vector.tensor_tensor(z, y[:], top[:].unsqueeze(1).to_broadcast([P, D, P]), ALU.subtract)
            e = ring.tile([P, D, P], F32, name="e")
            nc.scalar.activation(e[:], z, ACT.Exp)
            e2 = ring.tile([P, D, P], F32, name="e2")
            nc.scalar.activation(e2[:], z, ACT.Exp, scale=2.0)
            state[c, "e"] = e
            state[c, "e2"] = e2

        def group_sums(c):
            t, h = chunks[c]
            ey = ring.tile([P, D, P], F32, name="ey")
            nc.vector.tensor_tensor(ey[:], state[c, "y"][:], state[c, "e"][:], ALU.mult)
            if h == 0:
                state[t, "sums"] = sum_banks.tile([P, 2, V], F32, name="sums")
                state[t, "weighted"] = sum_banks.tile([P, 2, V], F32, name="weighted")
            cols = slice(h * P, (h + 1) * P)
            totals = [state[t, "sums"][:, 0, cols], state[t, "sums"][:, 1, cols], state[t, "weighted"][:, 0, cols]]
            if c == len(chunks) - 1:
                spare_sums = score_banks.tile([P, D, P], F32, name="bank")
                spare_weighted = score_banks.tile([P, D, P], F32, name="bank")
                totals = [spare_sums[:, 0, :], spare_sums[:, 1, :], spare_weighted[:, 0, :]]
            state[c, "totals"] = totals
            targets = zip((state[c, "e"], state[c, "e2"], ey), totals)
            for terms, total in targets:
                for d in range(D):
                    nc.tensor.matmul(total, terms[:, d, :], ident[:], start=(d == 0), stop=(d == D - 1), is_transpose=True)

        def last_ratios(h):
            t = PACK - 1
            sum_e, sum_e2, sum_ey = state[HALVES * t + h, "totals"]
            sum_sq = ring.tile([P, P], F32, name="sum_sq")
            nc.scalar.activation(sum_sq[:], sum_e, ACT.Square)
            sum_twice = ring.tile([P, P], F32, name="sum_twice")
            nc.scalar.activation(sum_twice[:], sum_e, ACT.Copy, scale=2.0)
            if h == 0:
                state[t, "window"] = keep.tile([P, 4 * V], F32, name="window%d" % t)
            ratio, num, den, crossed = [state[t, "window"][:, n * V + h * P : n * V + (h + 1) * P] for n in range(4)]
            nc.vector.scalar_tensor_tensor(den, sum_e2, 2.0, sum_sq[:], ALU.mult, ALU.add)
            nc.vector.scalar_tensor_tensor(num, sum_ey, unit_sb[:, t : t + 1], sum_twice[:], ALU.mult, ALU.mult)
            halves = lambda ap: ap.rearrange("p (a b) -> p a b", a=2)
            pairs = ring.tile([P, P // 2], F32, name="pairs")
            inv_pairs = ring.tile([P, P // 2], F32, name="inv_pairs")
            nc.vector.tensor_tensor(pairs[:], den[:, : P // 2], den[:, P // 2 :], ALU.mult)
            nc.vector.reciprocal(inv_pairs[:], pairs[:])
            nc.vector.tensor_tensor(halves(crossed), halves(num), halves(den)[:, ::-1, :], ALU.mult)
            nc.vector.tensor_tensor(halves(ratio), halves(crossed), inv_pairs[:].unsqueeze(1).to_broadcast([P, 2, P // 2]), ALU.mult)

        def ratios(t):
            sums, weighted = state[t, "sums"], state[t, "weighted"]
            spent = state[SQUARE_AFTER[t], "z"].rearrange("p d f -> p (d f)")
            sum_sq, sum_twice = spent[:, :V], spent[:, V:]
            nc.scalar.activation(sum_sq, sums[:, 0, :], ACT.Square)
            nc.scalar.activation(sum_twice, sums[:, 0, :], ACT.Copy, scale=2.0)
            window = keep.tile([P, 4 * V], F32, name="window%d" % t)
            ratio, num, den, crossed = [window[:, n * V : (n + 1) * V] for n in range(4)]
            nc.vector.scalar_tensor_tensor(den, sums[:, 1, :], 2.0, sum_sq[:], ALU.mult, ALU.add)
            nc.vector.scalar_tensor_tensor(num, weighted[:, 0, :], unit_sb[:, t : t + 1], sum_twice[:], ALU.mult, ALU.mult)
            products = nc.gpsimd if t < GPSIMD_TILES else nc.vector
            halves = lambda ap: ap.rearrange("p (a b) -> p a b", a=2)
            pairs = ring.tile([P, V // 2], F32, name="pairs")
            quads = ring.tile([P, V // 4], F32, name="quads")
            inv_quads = state[INVERT_AFTER[t], "top"][:, (t % 2) * V // 4 : (t % 2 + 1) * V // 4]
            inv_pairs = ring.tile([P, V // 2], F32, name="inv_pairs")
            products.tensor_tensor(pairs[:], den[:, : V // 2], den[:, V // 2 :], ALU.mult)
            products.tensor_tensor(quads[:], pairs[:, : V // 4], pairs[:, V // 4 :], ALU.mult)
            products.tensor_tensor(halves(crossed), halves(num), halves(den)[:, ::-1, :], ALU.mult)
            nc.vector.reciprocal(inv_quads[:], quads[:])
            products.tensor_tensor(
                halves(inv_pairs[:]), halves(pairs[:])[:, ::-1, :], inv_quads[:].unsqueeze(1).to_broadcast([P, 2, V // 4]), ALU.mult
            )
            products.tensor_tensor(halves(ratio), halves(crossed), inv_pairs[:].unsqueeze(1).to_broadcast([P, 2, V // 2]), ALU.mult)
            state[t, "window"] = window

        def fetch(t):
            window = state[t, "window"]
            if t < PACK - 1:
                nc.scalar.activation(fetched[:, t, :], window[:].indirect(use_sb[:]), ACT.Copy)
            else:
                for lo, hi in pieces:
                    nc.scalar.activation(fetched[:, t, lo:hi], window[:].indirect(use_sb[:, lo // LIST_ROWS : hi // LIST_ROWS]), ACT.Copy)

        last = len(chunks) - 1
        scores(0)
        for step in range(len(chunks) + LAG):
            if step < last:
                scores(step + 1)
            if step <= last:
                exponentials(step)
            c = step - LAG
            if c >= 0:
                group_sums(c)
            for t in range(PACK - 1):
                if min(step, last) == last or step == INVERT_AFTER[t]:
                    if (t, "window") not in state and c >= HALVES * t + 1:
                        ratios(t)
            if c >= 0 and chunks[c][0] == PACK - 1:
                last_ratios(chunks[c][1])
        nc.vector.quantize_mx(out=w1_codes[:].bitcast(FP8X4), scales=w1_scales[:], in_=w1_bf[:])
        for t in range(PACK):
            fetch(t)

        for r0, r1 in pieces:
            piece = r1 - r0
            hid_bf = ring.tile([P, piece * PACK], BF16, name="hid_bf", align_bytes=64)
            nc.vector.tensor_tensor(
                hid_bf[:].rearrange("p (c i t) -> p c t i", i=4, t=PACK),
                fetched[:, :, r0 : r0 + piece].rearrange("p t (c i) -> p c t i", i=4),
                tgt_scaled[:, :, r0 : r0 + piece].rearrange("p t (c i) -> p c t i", i=4),
                ALU.subtract,
            )
            hid_codes = ring.tile([P, piece], U32, name="hid_codes", align_bytes=64)
            hid_scales = ring.tile([P, piece], U8, name="hid_scales", align_bytes=64)
            nc.vector.quantize_mx(out=hid_codes[:].bitcast(FP8X4), scales=hid_scales[:], in_=hid_bf[:])
            acc = score_banks.tile([P, N // P, piece], F32, name="bank")
            for mh in range(N // P):
                nc.tensor.matmul_mx(
                    out=acc[:, mh, :],
                    lhsT=w1_codes[:, mh * P : (mh + 1) * P].bitcast(FP8X4),
                    lhsT_scale=w1_scales[:, mh * P : (mh + 1) * P],
                    rhs=hid_codes[:].bitcast(FP8X4),
                    rhs_scale=hid_scales[:],
                    start=True,
                    stop=True,
                )
            result = ring.tile([P, N // P, piece], F32, name="result")
            nc.scalar.copy(result[:], acc[:])
            nc.sync.dma_start(out=out[:, r0 : r0 + piece].rearrange("(h p) r -> p h r", p=P), in_=result[:])
